import numpy as np
import ml_dtypes


def mxq(x, axis, fmt="e4m3"):
    dtype, down = {"e4m3": (ml_dtypes.float8_e4m3fn, 7), "e5m2": (ml_dtypes.float8_e5m2, 14)}[fmt]
    v = np.moveaxis(np.asarray(x, np.float32).astype(ml_dtypes.bfloat16).astype(np.float64), axis, -1)
    blocks = v.reshape(v.shape[:-1] + (-1, 32))
    amax = np.abs(blocks).max(-1, keepdims=True)
    byte = np.maximum(np.where(amax > 0, np.frexp(amax)[1] - 1 + 127, 0) - down, 1)
    scale = np.exp2(byte - 127.0)
    codes = (blocks / scale).astype(np.float32).astype(dtype).astype(np.float64)
    return np.moveaxis((codes * scale).reshape(v.shape), -1, axis)


WIDE = False


def mx_kscale(k):
    if not WIDE:
        return np.ones(k)
    levels = np.array([10, -10, 5, -5, 0])
    if k % 512:
        return np.exp2(np.random.permutation(np.resize(levels, k // 32))).repeat(32)
    a = np.empty((k // 512, 16))
    for p in range(k // 512):
        a[p, :8] = np.random.permutation(np.resize(levels, 8))
        for g in range(8):
            far = levels[np.abs(levels - a[p, g]) >= 10]
            a[p, g + 8] = far[np.random.randint(len(far))]
    return np.exp2(a.ravel()).repeat(32)


def f64(x):
    return np.asarray(x).astype(np.float64)


def striped(idx):
    return np.tile(idx.reshape(-1, 16).T, (8, 1)).astype(np.uint16)


def unstriped(offs):
    return offs[:16].T.reshape(-1).astype(np.int64)


def relu(v):
    return np.maximum(v, 0.0)


K, T, D, V, H, N = 2048, 1024, 6, 512, 1024, 512
P = 2 ** 7


def setup_inputs():
    n = np.random.standard_normal
    s = mx_kscale(K)[:, None]
    u = mx_kscale(H)
    return {
        "xT": (n((K, T)) * s).astype(np.float32),
        "w1": (n((K, H)) / np.sqrt(K) / s * u).astype(np.float32),
        "w2": (n((H, N)) / np.sqrt(H) / u[:, None]).astype(np.float32),
        "gate": np.tile(np.random.uniform(0.2, 1.0, (D, 1, V)) / np.sqrt(D), (1, P, 1)).astype(np.float32),
        "pos1": striped(np.random.permutation(T)[:V]),
        "pos2": striped(np.random.permutation(T)[:V]),
        "pos3": striped(np.random.permutation(T)[:V]),
        "pos4": striped(np.random.permutation(T)[:V]),
        "pos5": striped(np.random.permutation(T)[:V]),
        "pos6": striped(np.random.permutation(T)[:V]),
    }


def reference(xT, w1, w2, gate, pos1, pos2, pos3, pos4, pos5, pos6):
    h = relu(mxq(f64(w1), 0, "e4m3").T @ mxq(f64(xT), 0, "e4m3"))
    z = sum(f64(gate)[d, :1] * h[:, unstriped(p)] for d, p in enumerate((pos1, pos2, pos3, pos4, pos5, pos6)))
    return mxq(f64(w2), 0, "e4m3").T @ mxq(z, 0, "e4m3")

@@ -1,0 +1,265 @@
+from contextlib import ExitStack
+
+import concourse.mybir as mybir
+from concourse.masks import make_identity
+
+K, T, D, V, H, N = 2048, 1024, 6, 512, 1024, 512
+FLOPS = 2 * K * T * H + 2 * H * V * N + 2 * D * V * H
+
+F32 = mybir.dt.float32
+BF16 = mybir.dt.bfloat16
+U32 = mybir.dt.uint32
+U16 = mybir.dt.uint16
+U8 = mybir.dt.uint8
+FP8X4 = mybir.dt.float8_e4m3fn_x4
+RELU = mybir.ActivationFunctionType.Relu
+MULT = mybir.AluOpType.mult
+
+P = 128
+J = 4
+KP = P * J
+G1 = K // KP
+G2 = H // KP
+NB = H // P
+BG = NB // G2
+NC = V // P
+HALF = 512
+SC = 160
+
+
+def tile_picked_gcn_mlp_relu_sub_l_kernel(tc, xT, w1, w2, gate, pos1, pos2, pos3, pos4, pos5, pos6, out):
+    nc = tc.nc
+    with ExitStack() as ctx:
+        lists = ctx.enter_context(tc.tile_pool(name="lists", bufs=1))
+        keep = ctx.enter_context(tc.tile_pool(name="keep", bufs=1))
+        rawx_pool = ctx.enter_context(tc.tile_pool(name="rawx", bufs=4))
+        raww_pool = ctx.enter_context(tc.tile_pool(name="raww", bufs=3))
+        xin_pool = ctx.enter_context(tc.tile_pool(name="xin", bufs=2))
+        win_pool = ctx.enter_context(tc.tile_pool(name="win", bufs=2))
+        wq_pool = ctx.enter_context(tc.tile_pool(name="wq", bufs=3))
+        h_pool = ctx.enter_context(tc.tile_pool(name="h", bufs=3))
+        prod_pool = ctx.enter_context(tc.tile_pool(name="prod", bufs=2))
+        zts_pool = ctx.enter_context(tc.tile_pool(name="zts", bufs=2))
+        zin_pool = ctx.enter_context(tc.tile_pool(name="zin", bufs=3))
+        res_pool = ctx.enter_context(tc.tile_pool(name="res", bufs=4))
+        acc_pool = ctx.enter_context(tc.psum_pool(name="acc", bufs=4))
+        zt_pool = ctx.enter_context(tc.psum_pool(name="zt", bufs=2))
+        zb_pool = ctx.enter_context(tc.psum_pool(name="zb", bufs=2))
+
+        dummy = keep.tile([P, 2], F32, name="dummy")
+        nc.gpsimd.memset(dummy[:], 0.0)
+        dummy2 = keep.tile([P, 2], F32, name="dummy2")
+        nc.scalar.activation(dummy2[:], dummy[:], RELU)
+        ident = keep.tile([P, P], F32, name="ident")
+        make_identity(nc, ident[:])
+
+        gates = [keep.tile([P, V], F32, name=f"gate{d}") for d in range(D)]
+        pos = [lists.tile([P, V // 16], U16, name=f"pos{d}") for d in range(D)]
+        xcodes = [keep.tile([P, T], U32, name=f"xcodes{g}", align_bytes=64) for g in range(G1)]
+        xscales = [keep.tile([P, T], U8, name=f"xscales{g}", align_bytes=64) for g in range(G1)]
+        w2codes = [keep.tile([P, N], U32, name=f"w2codes{g}", align_bytes=64) for g in range(G2)]
+        w2scales = [keep.tile([P, N], U8, name=f"w2scales{g}", align_bytes=64) for g in range(G2)]
+        zcodes = [keep.tile([P, V], U32, name=f"zcodes{g}", align_bytes=64) for g in range(G2)]
+        zscales = [keep.tile([P, V], U8, name=f"zscales{g}", align_bytes=64) for g in range(G2)]
+
+        raww = {}
+
+        def load_w1_pass(b, g):
+            if g == 0:
+                raww[b] = raww_pool.tile([P, G1, J, P], F32, name="raw_w1")
+            nc.sync.dma_start(
+                out=raww[b][:, g],
+                in_=w1[g * KP : (g + 1) * KP, b * P : (b + 1) * P].rearrange("(p j) c -> p j c", j=J),
+            )
+
+        rawx = {}
+
+        def load_x(g, t0, t1):
+            if t0 == 0:
+                rawx[g] = rawx_pool.tile([P, J, T], F32, name="raw_x")
+            nc.sync.dma_start(
+                out=rawx[g][:, :, t0:t1],
+                in_=xT[g * KP : (g + 1) * KP, t0:t1].rearrange("(p j) t -> p j t", j=J),
+            )
+
+        def load_gate(d):
+            nc.sync.dma_start(out=gates[d][:], in_=gate[d])
+
+        load_x(0, 0, HALF)
+        load_x(0, HALF, T)
+        for g in range(G1):
+            load_w1_pass(0, g)
+        load_x(1, 0, T)
+        load_x(2, 0, T)
+        for d, p in enumerate((pos1, pos2, pos3, pos4, pos5, pos6)):
+            nc.sync.dma_start(pos[d][:], p)
+        load_x(3, 0, HALF)
+        load_x(3, HALF, T)
+        load_gate(0)
+        load_w1_pass(1, 0)
+        load_gate(1)
+        load_w1_pass(1, 1)
+        load_gate(2)
+        load_w1_pass(1, 2)
+        load_w1_pass(1, 3)
+        for d in range(3, D):
+            load_gate(d)
+
+        wq = {}
+
+        def quantize_w1(b):
+            inter = win_pool.tile([P, G1, P, J], BF16, name="w1_in", align_bytes=64)
+            codes = wq_pool.tile([P, G1 * P], U32, name="w1_codes", align_bytes=64)
+            scales = wq_pool.tile([P, G1 * P], U8, name="w1_scales", align_bytes=64)
+            for g in range(G1):
+                nc.scalar.copy(out=inter[:, g], in_=raww[b][:, g].rearrange("p j c -> p c j"))
+            for q in range(2):
+                nc.vector.quantize_mx(
+                    out=codes[:, q * 256 : (q + 1) * 256].bitcast(FP8X4),
+                    scales=scales[:, q * 256 : (q + 1) * 256],
+                    in_=inter[:, 2 * q : 2 * q + 2].rearrange("p g c j -> p (g c j)"),
+                )
+            wq[b] = (codes, scales)
+
+        def quantize_x(g, half):
+            if half == 0:
+                rawx[g, "in"] = xin_pool.tile([P, T, J], BF16, name="x_in", align_bytes=64)
+            inter = rawx[g, "in"]
+            lo, mid, hi = half * HALF, half * HALF + SC, (half + 1) * HALF
+            nc.scalar.copy(out=inter[:, lo:mid], in_=rawx[g][:, :, lo:mid].rearrange("p j t -> p t j"))
+            nc.vector.tensor_copy(out=inter[:, mid:hi], in_=rawx[g][:, :, mid:hi].rearrange("p j t -> p t j"))
+            nc.vector.quantize_mx(
+                out=xcodes[g][:, lo:hi].bitcast(FP8X4),
+                scales=xscales[g][:, lo:hi],
+                in_=inter[:, lo:hi].rearrange("p t j -> p (t j)"),
+            )
+
+        hs = {}
+
+        def layer1(b, order):
+            codes, scales = wq[b]
+            acc = [acc_pool.tile([P, HALF], F32, name="acc") for s in range(2)]
+            for g, s in order:
+                cols = slice(g * P, (g + 1) * P)
+                ts = slice(s * HALF, (s + 1) * HALF)
+                nc.tensor.matmul_mx(
+                    out=acc[s][:],
+                    lhsT=codes[:, cols].bitcast(FP8X4),
+                    lhsT_scale=scales[:, cols],
+                    rhs=xcodes[g][:, ts].bitcast(FP8X4),
+                    rhs_scale=xscales[g][:, ts],
+                    start=(g == 0),
+                    stop=(g == G1 - 1),
+                )
+            h = h_pool.tile([P, T], F32, name="h")
+            for s in range(2):
+                nc.scalar.activation(h[:, s * HALF : (s + 1) * HALF], acc[s][:], RELU)
+            hs[b] = h
+
+        def gather(b, v0, n, tag):
+            prods = []
+            for d in range(D):
+                prod = prod_pool.tile([P, n], F32, name=f"prod{d}_{tag}")
+                nc.vector.tensor_tensor(
+                    prod[:], hs[b][:].indirect(pos[d][:, v0 // 16 : (v0 + n) // 16]), gates[d][:, v0 : v0 + n], MULT
+                )
+                prods.append(prod)
+            return prods
+
+        zts = {}
+
+        def sum_transposed(b, prods, c0, engine_copy):
+            g, bl = b // BG, b % BG
+            if bl == 0:
+                zts[g] = zts_pool.tile([P, NC, J, P], F32, name="zts")
+            n = prods[0].shape[1] // P
+            zt = zt_pool.tile([P, n, P], F32, name="zt")
+            for c in range(n):
+                for d in range(D):
+                    nc.tensor.matmul(
+                        zt[:, c], prods[d][:, c * P : (c + 1) * P], ident[:],
+                        start=(d == 0), stop=(d == D - 1), is_transpose=True,
+                    )
+            q = P // J
+            engine_copy(
+                out=zts[g][:, c0 : c0 + n, :, bl * q : (bl + 1) * q],
+                in_=zt[:].rearrange("p c (q t) -> p c t q", t=J),
+            )
+
+        def quantize_z(g, c):
+            zb = zb_pool.tile([P, J, P], F32, name="zb")
+            for t in range(J):
+                nc.tensor.transpose(zb[:, t], zts[g][:, c, t], ident[:])
+            inter = zin_pool.tile([P, P, J], BF16, name="z_in", align_bytes=64)
+            nc.scalar.copy(out=inter[:], in_=zb[:].rearrange("p t v -> p v t"))
+            nc.vector.quantize_mx(
+                out=zcodes[g][:, c * P : (c + 1) * P].bitcast(FP8X4),
+                scales=zscales[g][:, c * P : (c + 1) * P],
+                in_=inter[:].rearrange("p v t -> p (v t)"),
+            )
+
+        def quantize_w2():
+            raw = rawx_pool.tile([P, G2, J, N], F32, name="raw_x")
+            for g in range(G2):
+                nc.sync.dma_start(out=raw[:, g], in_=w2[g * KP : (g + 1) * KP].rearrange("(p j) m -> p j m", j=J))
+            inter = xin_pool.tile([P, G2, N, J], BF16, name="x_in", align_bytes=64)
+            for g in range(G2):
+                nc.scalar.copy(out=inter[:, g], in_=raw[:, g].rearrange("p j m -> p m j"))
+                nc.vector.quantize_mx(
+                    out=w2codes[g][:].bitcast(FP8X4),
+                    scales=w2scales[g][:],
+                    in_=inter[:, g].rearrange("p m j -> p (m j)"),
+                )
+
+        out_v = out.rearrange("(m p) v -> p m v", p=P)
+
+        def layer2(v0, n, m0, m1, engine_copy):
+            acc = acc_pool.tile([P, m1 - m0, n], F32, name="acc")
+            for m in range(m0, m1):
+                for g in range(G2):
+                    nc.tensor.matmul_mx(
+                        out=acc[:, m - m0],
+                        lhsT=w2codes[g][:, m * P : (m + 1) * P].bitcast(FP8X4),
+                        lhsT_scale=w2scales[g][:, m * P : (m + 1) * P],
+                        rhs=zcodes[g][:, v0 : v0 + n].bitcast(FP8X4),
+                        rhs_scale=zscales[g][:, v0 : v0 + n],
+                        start=(g == 0),
+                        stop=(g == G2 - 1),
+                    )
+            res = res_pool.tile([P, m1 - m0, n], F32, name="res")
+            engine_copy(out=res[:], in_=acc[:])
+            nc.sync.dma_start(out=out_v[:, m0:m1, v0 : v0 + n], in_=res[:])
+
+        quantize_w1(0)
+        for g in range(G1):
+            for half in range(2):
+                quantize_x(g, half)
+        layer1(0, [(g, s) for g in range(G1) for s in range(2)])
+
+        for b in range(NB):
+            if b + 2 < NB:
+                for g in range(G1):
+                    load_w1_pass(b + 2, g)
+            if b + 1 < NB:
+                quantize_w1(b + 1)
+                layer1(b + 1, [(g, s) for s in range(2) for g in range(G1)])
+            if b == 3:
+                quantize_w2()
+            if b < NB - 1:
+                sum_transposed(b, gather(b, 0, V, "a"), 0, nc.scalar.copy)
+            if b == BG:
+                for c in range(NC):
+                    quantize_z(0, c)
+
+        first = gather(NB - 1, 0, 3 * P, "a")
+        sum_transposed(NB - 1, first, 0, nc.scalar.copy)
+        for c in range(3):
+            quantize_z(1, c)
+        last = gather(NB - 1, 3 * P, P, "b")
+        layer2(0, 2 * P, 0, 2, nc.scalar.copy)
+        layer2(0, 2 * P, 2, 4, nc.scalar.copy)
+        layer2(2 * P, P, 0, 4, nc.scalar.copy)
+        sum_transposed(NB - 1, last, 3, nc.vector.tensor_copy)
+        quantize_z(1, 3)
+        layer2(3 * P, P, 0, 2, nc.scalar.copy)
+        layer2(3 * P, P, 2, 4, nc.vector.tensor_copy)

@@ -57,8 +57,8 @@ def tile_picked_gcn_mlp_relu_sub_l_kernel(tc, xT, w1, w2, gate, pos1, pos2, pos3
         pos = [lists.tile([P, V // 16], U16, name=f"pos{d}") for d in range(D)]
         xcodes = [keep.tile([P, T], U32, name=f"xcodes{g}", align_bytes=64) for g in range(G1)]
         xscales = [keep.tile([P, T], U8, name=f"xscales{g}", align_bytes=64) for g in range(G1)]
-        w2codes = [keep.tile([P, N], U32, name=f"w2codes{g}", align_bytes=64) for g in range(G2)]
-        w2scales = [keep.tile([P, N], U8, name=f"w2scales{g}", align_bytes=64) for g in range(G2)]
+        w2codes = keep.tile([P, G2 * N], U32, name="w2codes", align_bytes=64)
+        w2scales = keep.tile([P, G2 * N], U8, name="w2scales", align_bytes=64)
         zcodes = [keep.tile([P, V], U32, name=f"zcodes{g}", align_bytes=64) for g in range(G2)]
         zscales = [keep.tile([P, V], U8, name=f"zscales{g}", align_bytes=64) for g in range(G2)]
 
@@ -85,41 +85,58 @@ def tile_picked_gcn_mlp_relu_sub_l_kernel(tc, xT, w1, w2, gate, pos1, pos2, pos3
         def load_gate(d):
             nc.sync.dma_start(out=gates[d][:], in_=gate[d])
 
-        load_x(0, 0, HALF)
-        load_x(0, HALF, T)
-        for g in range(G1):
-            load_w1_pass(0, g)
+        def load_pos(d):
+            nc.sync.dma_start(pos[d][:], (pos1, pos2, pos3, pos4, pos5, pos6)[d])
+
+        load_x(0, 0, T)
+        load_w1_pass(0, 0)
+        load_w1_pass(0, 1)
         load_x(1, 0, T)
         load_x(2, 0, T)
-        for d, p in enumerate((pos1, pos2, pos3, pos4, pos5, pos6)):
-            nc.sync.dma_start(pos[d][:], p)
+        load_pos(0)
         load_x(3, 0, HALF)
         load_x(3, HALF, T)
+        load_w1_pass(0, 2)
+        load_w1_pass(0, 3)
         load_gate(0)
+        load_pos(1)
         load_w1_pass(1, 0)
         load_gate(1)
+        load_pos(2)
         load_w1_pass(1, 1)
         load_gate(2)
+        load_pos(3)
         load_w1_pass(1, 2)
+        load_gate(3)
+        load_pos(4)
         load_w1_pass(1, 3)
-        for d in range(3, D):
-            load_gate(d)
+        load_gate(4)
+        load_pos(5)
+        load_gate(5)
 
         wq = {}
 
-        def quantize_w1(b):
-            inter = win_pool.tile([P, G1, P, J], BF16, name="w1_in", align_bytes=64)
-            codes = wq_pool.tile([P, G1 * P], U32, name="w1_codes", align_bytes=64)
-            scales = wq_pool.tile([P, G1 * P], U8, name="w1_scales", align_bytes=64)
-            for g in range(G1):
-                nc.scalar.copy(out=inter[:, g], in_=raww[b][:, g].rearrange("p j c -> p c j"))
-            for q in range(2):
-                nc.vector.quantize_mx(
-                    out=codes[:, q * 256 : (q + 1) * 256].bitcast(FP8X4),
-                    scales=scales[:, q * 256 : (q + 1) * 256],
-                    in_=inter[:, 2 * q : 2 * q + 2].rearrange("p g c j -> p (g c j)"),
-                )
-            wq[b] = (codes, scales)
+        win = {}
+
+        def interleave_w1(b, g, split=0):
+            if g == 0:
+                win[b] = win_pool.tile([P, G1, P, J], BF16, name="w1_in", align_bytes=64)
+            src = raww[b][:, g].rearrange("p j c -> p c j")
+            if split:
+                nc.vector.tensor_copy(out=win[b][:, g, :split], in_=src[:, :split])
+            nc.scalar.copy(out=win[b][:, g, split:], in_=src[:, split:])
+
+        def quantize_w1(b, g, n):
+            if g == 0:
+                codes = wq_pool.tile([P, G1 * P], U32, name="w1_codes", align_bytes=64)
+                scales = wq_pool.tile([P, G1 * P], U8, name="w1_scales", align_bytes=64)
+                wq[b] = (codes, scales)
+            codes, scales = wq[b]
+            nc.vector.quantize_mx(
+                out=codes[:, g * P : (g + n) * P].bitcast(FP8X4),
+                scales=scales[:, g * P : (g + n) * P],
+                in_=win[b][:, g : g + n].rearrange("p g c j -> p (g c j)"),
+            )
 
         def quantize_x(g, half):
             if half == 0:
@@ -153,18 +170,19 @@ def tile_picked_gcn_mlp_relu_sub_l_kernel(tc, xT, w1, w2, gate, pos1, pos2, pos3
                 )
             h = h_pool.tile([P, T], F32, name="h")
             for s in range(2):
-                nc.scalar.activation(h[:, s * HALF : (s + 1) * HALF], acc[s][:], RELU)
+                if b == 0 and s == 1:
+                    nc.vector.tensor_scalar_max(h[:, HALF:T], acc[1][:], 0.0)
+                else:
+                    nc.scalar.activation(h[:, s * HALF : (s + 1) * HALF], acc[s][:], RELU)
             hs[b] = h
 
-        def gather(b, v0, n, tag):
-            prods = []
-            for d in range(D):
-                prod = prod_pool.tile([P, n], F32, name=f"prod{d}_{tag}")
+        def gather(b, v0, n, prods, ds):
+            for d in ds:
+                prod = prod_pool.tile([P, n], F32, name=f"prod{d}")
                 nc.vector.tensor_tensor(
                     prod[:], hs[b][:].indirect(pos[d][:, v0 // 16 : (v0 + n) // 16]), gates[d][:, v0 : v0 + n], MULT
                 )
                 prods.append(prod)
-            return prods
 
         zts = {}
 
@@ -173,43 +191,67 @@ def tile_picked_gcn_mlp_relu_sub_l_kernel(tc, xT, w1, w2, gate, pos1, pos2, pos3
             if bl == 0:
                 zts[g] = zts_pool.tile([P, NC, J, P], F32, name="zts")
             n = prods[0].shape[1] // P
-            zt = zt_pool.tile([P, n, P], F32, name="zt")
-            for c in range(n):
-                for d in range(D):
-                    nc.tensor.matmul(
-                        zt[:, c], prods[d][:, c * P : (c + 1) * P], ident[:],
-                        start=(d == 0), stop=(d == D - 1), is_transpose=True,
-                    )
             q = P // J
-            engine_copy(
-                out=zts[g][:, c0 : c0 + n, :, bl * q : (bl + 1) * q],
-                in_=zt[:].rearrange("p c (q t) -> p c t q", t=J),
-            )
+            if n == NC:
+                zt = zt_pool.tile([P, n, P], F32, name="zt")
+                for c in range(n):
+                    for d in range(D):
+                        nc.tensor.matmul(
+                            zt[:, c], prods[d][:, c * P : (c + 1) * P], ident[:],
+                            start=(d == 0), stop=(d == D - 1), is_transpose=True,
+                        )
+                engine_copy(
+                    out=zts[g][:, c0 : c0 + n, :, bl * q : (bl + 1) * q],
+                    in_=zt[:].rearrange("p c (q t) -> p c t q", t=J),
+                )
+            else:
+                banks = [zt_pool.tile([P, P], F32, name="zt") for c in range(n)]
+                for d in range(D):
+                    for c in range(n):
+                        nc.tensor.matmul(
+                            banks[c][:], prods[d][:, c * P : (c + 1) * P], ident[:],
+                            start=(d == 0), stop=(d == D - 1), is_transpose=True,
+                        )
+                for c in range(n):
+                    engine_copy(
+                        out=zts[g][:, c0 + c, :, bl * q : (bl + 1) * q],
+                        in_=banks[c][:].rearrange("p (q t) -> p t q", t=J),
+                    )
 
-        def quantize_z(g, c):
+        zin = {}
+
+        def untranspose_z(g, c, engine_copy):
+            if (g, c) in ((0, 0), (1, 0), (1, 2), (1, 3)):
+                zin[g] = zin_pool.tile([P, NC, P, J], BF16, name="z_in", align_bytes=64)
             zb = zb_pool.tile([P, J, P], F32, name="zb")
             for t in range(J):
                 nc.tensor.transpose(zb[:, t], zts[g][:, c, t], ident[:])
-            inter = zin_pool.tile([P, P, J], BF16, name="z_in", align_bytes=64)
-            nc.scalar.copy(out=inter[:], in_=zb[:].rearrange("p t v -> p v t"))
+            engine_copy(out=zin[g][:, c], in_=zb[:].rearrange("p t v -> p v t"))
+
+        def quantize_z(g, c, n):
             nc.vector.quantize_mx(
-                out=zcodes[g][:, c * P : (c + 1) * P].bitcast(FP8X4),
-                scales=zscales[g][:, c * P : (c + 1) * P],
-                in_=inter[:].rearrange("p v t -> p (v t)"),
+                out=zcodes[g][:, c * P : (c + n) * P].bitcast(FP8X4),
+                scales=zscales[g][:, c * P : (c + n) * P],
+                in_=zin[g][:, c : c + n].rearrange("p c v t -> p (c v t)"),
             )
 
-        def quantize_w2():
+        w2in = []
+
+        def interleave_w2():
             raw = rawx_pool.tile([P, G2, J, N], F32, name="raw_x")
             for g in range(G2):
                 nc.sync.dma_start(out=raw[:, g], in_=w2[g * KP : (g + 1) * KP].rearrange("(p j) m -> p j m", j=J))
             inter = xin_pool.tile([P, G2, N, J], BF16, name="x_in", align_bytes=64)
             for g in range(G2):
                 nc.scalar.copy(out=inter[:, g], in_=raw[:, g].rearrange("p j m -> p m j"))
-                nc.vector.quantize_mx(
-                    out=w2codes[g][:].bitcast(FP8X4),
-                    scales=w2scales[g][:],
-                    in_=inter[:, g].rearrange("p m j -> p (m j)"),
-                )
+            w2in.append(inter)
+
+        def quantize_w2():
+            nc.vector.quantize_mx(
+                out=w2codes[:].bitcast(FP8X4),
+                scales=w2scales[:],
+                in_=w2in[0][:].rearrange("p g m j -> p (g m j)"),
+            )
 
         out_v = out.rearrange("(m p) v -> p m v", p=P)
 
@@ -219,8 +261,8 @@ def tile_picked_gcn_mlp_relu_sub_l_kernel(tc, xT, w1, w2, gate, pos1, pos2, pos3
                 for g in range(G2):
                     nc.tensor.matmul_mx(
                         out=acc[:, m - m0],
-                        lhsT=w2codes[g][:, m * P : (m + 1) * P].bitcast(FP8X4),
-                        lhsT_scale=w2scales[g][:, m * P : (m + 1) * P],
+                        lhsT=w2codes[:, g * N + m * P : g * N + (m + 1) * P].bitcast(FP8X4),
+                        lhsT_scale=w2scales[:, g * N + m * P : g * N + (m + 1) * P],
                         rhs=zcodes[g][:, v0 : v0 + n].bitcast(FP8X4),
                         rhs_scale=zscales[g][:, v0 : v0 + n],
                         start=(g == 0),
@@ -230,36 +272,65 @@ def tile_picked_gcn_mlp_relu_sub_l_kernel(tc, xT, w1, w2, gate, pos1, pos2, pos3
             engine_copy(out=res[:], in_=acc[:])
             nc.sync.dma_start(out=out_v[:, m0:m1, v0 : v0 + n], in_=res[:])
 
-        quantize_w1(0)
+        interleave_w1(0, 0)
+        interleave_w1(0, 1)
         for g in range(G1):
             for half in range(2):
                 quantize_x(g, half)
+            if g == 1:
+                quantize_w1(0, 0, 2)
+        for g in (2, 3):
+            interleave_w1(0, g, split=80)
+            quantize_w1(0, g, 1)
         layer1(0, [(g, s) for g in range(G1) for s in range(2)])
 
-        for b in range(NB):
+        halves_first = [(g, s) for s in range(2) for g in range(G1)]
+        for b in range(NB - 1):
             if b + 2 < NB:
                 for g in range(G1):
                     load_w1_pass(b + 2, g)
-            if b + 1 < NB:
-                quantize_w1(b + 1)
-                layer1(b + 1, [(g, s) for s in range(2) for g in range(G1)])
+            for g in range(G1):
+                interleave_w1(b + 1, g)
+            prods = []
+            gather(b, 0, V, prods, range(0, 2))
+            if b == 0:
+                quantize_w1(1, 0, 2)
+                gather(b, 0, V, prods, range(2, 4))
+                quantize_w1(1, 2, 2)
+                layer1(1, [(g, s) for g in range(G1) for s in range(2)])
+                gather(b, 0, V, prods, range(4, D))
+            else:
+                quantize_w1(b + 1, 0, 4)
+                layer1(b + 1, halves_first)
+                gather(b, 0, V, prods, range(2, D))
             if b == 3:
-                quantize_w2()
-            if b < NB - 1:
-                sum_transposed(b, gather(b, 0, V, "a"), 0, nc.scalar.copy)
-            if b == BG:
+                interleave_w2()
+            if b == 4:
                 for c in range(NC):
-                    quantize_z(0, c)
+                    untranspose_z(0, c, nc.scalar.copy)
+            if b == 5:
+                quantize_z(0, 0, NC)
+                quantize_w2()
+            sum_transposed(b, prods, 0, nc.scalar.copy)
 
-        first = gather(NB - 1, 0, 3 * P, "a")
-        sum_transposed(NB - 1, first, 0, nc.scalar.copy)
-        for c in range(3):
-            quantize_z(1, c)
-        last = gather(NB - 1, 3 * P, P, "b")
+        b = NB - 1
+        p0, p1, p2 = [], [], []
+        gather(b, 0, 2 * P, p0, range(D))
+        sum_transposed(b, p0, 0, nc.scalar.copy)
+        gather(b, 2 * P, P, p1, range(D))
+        untranspose_z(1, 0, nc.scalar.copy)
+        untranspose_z(1, 1, nc.scalar.copy)
+        sum_transposed(b, p1, 2, nc.scalar.copy)
+        gather(b, 3 * P, P, p2, range(3))
+        quantize_z(1, 0, 2)
+        gather(b, 3 * P, P, p2, range(3, D))
+        untranspose_z(1, 2, nc.scalar.copy)
+        sum_transposed(b, p2, 3, nc.vector.tensor_copy)
+        quantize_z(1, 2, 1)
+        untranspose_z(1, 3, nc.scalar.copy)
+        quantize_z(1, 3, 1)
         layer2(0, 2 * P, 0, 2, nc.scalar.copy)
         layer2(0, 2 * P, 2, 4, nc.scalar.copy)
-        layer2(2 * P, P, 0, 4, nc.scalar.copy)
-        sum_transposed(NB - 1, last, 3, nc.vector.tensor_copy)
-        quantize_z(1, 3)
+        layer2(2 * P, P, 0, 4, nc.vector.tensor_copy)
         layer2(3 * P, P, 0, 2, nc.scalar.copy)
         layer2(3 * P, P, 2, 4, nc.vector.tensor_copy)

@@ -24,7 +24,6 @@ NB = H // P
 BG = NB // G2
 NC = V // P
 HALF = 512
-SC = 160
 
 
 def tile_picked_gcn_mlp_relu_sub_l_kernel(tc, xT, w1, w2, gate, pos1, pos2, pos3, pos4, pos5, pos6, out):
@@ -41,7 +40,7 @@ def tile_picked_gcn_mlp_relu_sub_l_kernel(tc, xT, w1, w2, gate, pos1, pos2, pos3
         prod_pool = ctx.enter_context(tc.tile_pool(name="prod", bufs=2))
         zts_pool = ctx.enter_context(tc.tile_pool(name="zts", bufs=2))
         zin_pool = ctx.enter_context(tc.tile_pool(name="zin", bufs=3))
-        res_pool = ctx.enter_context(tc.tile_pool(name="res", bufs=4))
+        res_pool = ctx.enter_context(tc.tile_pool(name="res", bufs=5))
         acc_pool = ctx.enter_context(tc.psum_pool(name="acc", bufs=4))
         zt_pool = ctx.enter_context(tc.psum_pool(name="zt", bufs=2))
         zb_pool = ctx.enter_context(tc.psum_pool(name="zb", bufs=2))
@@ -138,11 +137,11 @@ def tile_picked_gcn_mlp_relu_sub_l_kernel(tc, xT, w1, w2, gate, pos1, pos2, pos3
                 in_=win[b][:, g : g + n].rearrange("p g c j -> p (g c j)"),
             )
 
-        def quantize_x(g, half):
-            if half == 0:
+        def quantize_x(g, lo, hi):
+            if lo == 0:
                 rawx[g, "in"] = xin_pool.tile([P, T, J], BF16, name="x_in", align_bytes=64)
             inter = rawx[g, "in"]
-            lo, mid, hi = half * HALF, half * HALF + SC, (half + 1) * HALF
+            mid = lo + (hi - lo) * 5 // 16
             nc.scalar.copy(out=inter[:, lo:mid], in_=rawx[g][:, :, lo:mid].rearrange("p j t -> p t j"))
             nc.vector.tensor_copy(out=inter[:, mid:hi], in_=rawx[g][:, :, mid:hi].rearrange("p j t -> p t j"))
             nc.vector.quantize_mx(
@@ -189,9 +188,8 @@ def tile_picked_gcn_mlp_relu_sub_l_kernel(tc, xT, w1, w2, gate, pos1, pos2, pos3
         def sum_transposed(b, prods, c0, engine_copy):
             g, bl = b // BG, b % BG
             if bl == 0:
-                zts[g] = zts_pool.tile([P, NC, J, P], F32, name="zts")
+                zts[g] = zts_pool.tile([P, NC, KP], BF16, name="zts")
             n = prods[0].shape[1] // P
-            q = P // J
             if n == NC:
                 zt = zt_pool.tile([P, n, P], F32, name="zt")
                 for c in range(n):
@@ -200,10 +198,7 @@ def tile_picked_gcn_mlp_relu_sub_l_kernel(tc, xT, w1, w2, gate, pos1, pos2, pos3
                             zt[:, c], prods[d][:, c * P : (c + 1) * P], ident[:],
                             start=(d == 0), stop=(d == D - 1), is_transpose=True,
                         )
-                engine_copy(
-                    out=zts[g][:, c0 : c0 + n, :, bl * q : (bl + 1) * q],
-                    in_=zt[:].rearrange("p c (q t) -> p c t q", t=J),
-                )
+                engine_copy(out=zts[g][:, c0 : c0 + n, bl * P : (bl + 1) * P], in_=zt[:])
             else:
                 banks = [zt_pool.tile([P, P], F32, name="zt") for c in range(n)]
                 for d in range(D):
@@ -213,20 +208,22 @@ def tile_picked_gcn_mlp_relu_sub_l_kernel(tc, xT, w1, w2, gate, pos1, pos2, pos3
                             start=(d == 0), stop=(d == D - 1), is_transpose=True,
                         )
                 for c in range(n):
-                    engine_copy(
-                        out=zts[g][:, c0 + c, :, bl * q : (bl + 1) * q],
-                        in_=banks[c][:].rearrange("p (q t) -> p t q", t=J),
-                    )
+                    engine_copy(out=zts[g][:, c0 + c, bl * P : (bl + 1) * P], in_=banks[c][:])
 
         zin = {}
 
-        def untranspose_z(g, c, engine_copy):
+        def untranspose_z(g, c, n, engine_copy):
             if (g, c) in ((0, 0), (1, 0), (1, 2), (1, 3)):
                 zin[g] = zin_pool.tile([P, NC, P, J], BF16, name="z_in", align_bytes=64)
-            zb = zb_pool.tile([P, J, P], F32, name="zb")
-            for t in range(J):
-                nc.tensor.transpose(zb[:, t], zts[g][:, c, t], ident[:])
-            engine_copy(out=zin[g][:, c], in_=zb[:].rearrange("p t v -> p v t"))
+            zb = zb_pool.tile([P, n, 2, P], F32, name="zb")
+            for i in range(n):
+                words = zts[g][:, c + i].bitcast(F32)
+                for u in range(2):
+                    nc.tensor.transpose(zb[:, i, u], words[:, u::2], ident[:])
+            engine_copy(
+                out=zin[g][:, c : c + n].rearrange("p c v t -> p (c v t)").bitcast(F32).rearrange("p (c v u) -> p c v u", c=n, u=2),
+                in_=zb[:].rearrange("p c u v -> p c v u"),
+            )
 
         def quantize_z(g, c, n):
             nc.vector.quantize_mx(
@@ -276,7 +273,7 @@ def tile_picked_gcn_mlp_relu_sub_l_kernel(tc, xT, w1, w2, gate, pos1, pos2, pos3
         interleave_w1(0, 1)
         for g in range(G1):
             for half in range(2):
-                quantize_x(g, half)
+                quantize_x(g, half * HALF, (half + 1) * HALF)
             if g == 1:
                 quantize_w1(0, 0, 2)
         for g in (2, 3):
@@ -306,8 +303,8 @@ def tile_picked_gcn_mlp_relu_sub_l_kernel(tc, xT, w1, w2, gate, pos1, pos2, pos3
             if b == 3:
                 interleave_w2()
             if b == 4:
-                for c in range(NC):
-                    untranspose_z(0, c, nc.scalar.copy)
+                for c in range(0, NC, 2):
+                    untranspose_z(0, c, 2, nc.scalar.copy)
             if b == 5:
                 quantize_z(0, 0, NC)
                 quantize_w2()
@@ -318,19 +315,19 @@ def tile_picked_gcn_mlp_relu_sub_l_kernel(tc, xT, w1, w2, gate, pos1, pos2, pos3
         gather(b, 0, 2 * P, p0, range(D))
         sum_transposed(b, p0, 0, nc.scalar.copy)
         gather(b, 2 * P, P, p1, range(D))
-        untranspose_z(1, 0, nc.scalar.copy)
-        untranspose_z(1, 1, nc.scalar.copy)
+        untranspose_z(1, 0, 2, nc.scalar.copy)
         sum_transposed(b, p1, 2, nc.scalar.copy)
-        gather(b, 3 * P, P, p2, range(3))
+        gather(b, 3 * P, P, p2, range(0, 2))
         quantize_z(1, 0, 2)
-        gather(b, 3 * P, P, p2, range(3, D))
-        untranspose_z(1, 2, nc.scalar.copy)
-        sum_transposed(b, p2, 3, nc.vector.tensor_copy)
+        gather(b, 3 * P, P, p2, range(2, 5))
+        untranspose_z(1, 2, 1, nc.scalar.copy)
         quantize_z(1, 2, 1)
-        untranspose_z(1, 3, nc.scalar.copy)
-        quantize_z(1, 3, 1)
+        gather(b, 3 * P, P, p2, range(5, D))
+        sum_transposed(b, p2, 3, nc.vector.tensor_copy)
+        untranspose_z(1, 3, 1, nc.scalar.copy)
         layer2(0, 2 * P, 0, 2, nc.scalar.copy)
         layer2(0, 2 * P, 2, 4, nc.scalar.copy)
+        quantize_z(1, 3, 1)
         layer2(2 * P, P, 0, 4, nc.vector.tensor_copy)
         layer2(3 * P, P, 0, 2, nc.scalar.copy)
         layer2(3 * P, P, 2, 4, nc.vector.tensor_copy)

from contextlib import ExitStack

import concourse.mybir as mybir
from concourse.masks import make_identity

K, T, D, V, H, N = 2048, 1024, 6, 512, 1024, 512
FLOPS = 2 * K * T * H + 2 * H * V * N + 2 * D * V * H

F32 = mybir.dt.float32
BF16 = mybir.dt.bfloat16
U32 = mybir.dt.uint32
U16 = mybir.dt.uint16
U8 = mybir.dt.uint8
FP8X4 = mybir.dt.float8_e4m3fn_x4
RELU = mybir.ActivationFunctionType.Relu
MULT = mybir.AluOpType.mult

P = 128
J = 4
KP = P * J
G1 = K // KP
G2 = H // KP
NB = H // P
BG = NB // G2
NC = V // P
HALF = 512


def tile_picked_gcn_mlp_relu_sub_l_kernel(tc, xT, w1, w2, gate, pos1, pos2, pos3, pos4, pos5, pos6, out):
    nc = tc.nc
    with ExitStack() as ctx:
        lists = ctx.enter_context(tc.tile_pool(name="lists", bufs=1))
        keep = ctx.enter_context(tc.tile_pool(name="keep", bufs=1))
        rawx_pool = ctx.enter_context(tc.tile_pool(name="rawx", bufs=4))
        raww_pool = ctx.enter_context(tc.tile_pool(name="raww", bufs=3))
        xin_pool = ctx.enter_context(tc.tile_pool(name="xin", bufs=2))
        win_pool = ctx.enter_context(tc.tile_pool(name="win", bufs=2))
        wq_pool = ctx.enter_context(tc.tile_pool(name="wq", bufs=3))
        h_pool = ctx.enter_context(tc.tile_pool(name="h", bufs=3))
        prod_pool = ctx.enter_context(tc.tile_pool(name="prod", bufs=2))
        zts_pool = ctx.enter_context(tc.tile_pool(name="zts", bufs=2))
        zin_pool = ctx.enter_context(tc.tile_pool(name="zin", bufs=3))
        res_pool = ctx.enter_context(tc.tile_pool(name="res", bufs=5))
        acc_pool = ctx.enter_context(tc.psum_pool(name="acc", bufs=4))
        zt_pool = ctx.enter_context(tc.psum_pool(name="zt", bufs=2))
        zb_pool = ctx.enter_context(tc.psum_pool(name="zb", bufs=2))

        dummy = keep.tile([P, 2], F32, name="dummy")
        nc.gpsimd.memset(dummy[:], 0.0)
        dummy2 = keep.tile([P, 2], F32, name="dummy2")
        nc.scalar.activation(dummy2[:], dummy[:], RELU)
        ident = keep.tile([P, P], F32, name="ident")
        make_identity(nc, ident[:])

        gates = [keep.tile([P, V], F32, name=f"gate{d}") for d in range(D)]
        pos = [lists.tile([P, V // 16], U16, name=f"pos{d}") for d in range(D)]
        xcodes = [keep.tile([P, T], U32, name=f"xcodes{g}", align_bytes=64) for g in range(G1)]
        xscales = [keep.tile([P, T], U8, name=f"xscales{g}", align_bytes=64) for g in range(G1)]
        w2codes = keep.tile([P, G2 * N], U32, name="w2codes", align_bytes=64)
        w2scales = keep.tile([P, G2 * N], U8, name="w2scales", align_bytes=64)
        zcodes = [keep.tile([P, V], U32, name=f"zcodes{g}", align_bytes=64) for g in range(G2)]
        zscales = [keep.tile([P, V], U8, name=f"zscales{g}", align_bytes=64) for g in range(G2)]

        raww = {}

        def load_w1_pass(b, g):
            if g == 0:
                raww[b] = raww_pool.tile([P, G1, J, P], F32, name="raw_w1")
            nc.sync.dma_start(
                out=raww[b][:, g],
                in_=w1[g * KP : (g + 1) * KP, b * P : (b + 1) * P].rearrange("(p j) c -> p j c", j=J),
            )

        rawx = {}

        def load_x(g, t0, t1):
            if t0 == 0:
                rawx[g] = rawx_pool.tile([P, J, T], F32, name="raw_x")
            nc.sync.dma_start(
                out=rawx[g][:, :, t0:t1],
                in_=xT[g * KP : (g + 1) * KP, t0:t1].rearrange("(p j) t -> p j t", j=J),
            )

        def load_gate(d):
            nc.sync.dma_start(out=gates[d][:], in_=gate[d])

        def load_pos(d):
            nc.sync.dma_start(pos[d][:], (pos1, pos2, pos3, pos4, pos5, pos6)[d])

        load_x(0, 0, T)
        load_w1_pass(0, 0)
        load_w1_pass(0, 1)
        load_x(1, 0, T)
        load_x(2, 0, T)
        load_pos(0)
        load_x(3, 0, HALF)
        load_x(3, HALF, T)
        load_w1_pass(0, 2)
        load_w1_pass(0, 3)
        load_gate(0)
        load_pos(1)
        load_w1_pass(1, 0)
        load_gate(1)
        load_pos(2)
        load_w1_pass(1, 1)
        load_gate(2)
        load_pos(3)
        load_w1_pass(1, 2)
        load_gate(3)
        load_pos(4)
        load_w1_pass(1, 3)
        load_gate(4)
        load_pos(5)
        load_gate(5)

        wq = {}

        win = {}

        def interleave_w1(b, g, split=0):
            if g == 0:
                win[b] = win_pool.tile([P, G1, P, J], BF16, name="w1_in", align_bytes=64)
            src = raww[b][:, g].rearrange("p j c -> p c j")
            if split:
                nc.vector.tensor_copy(out=win[b][:, g, :split], in_=src[:, :split])
            nc.scalar.copy(out=win[b][:, g, split:], in_=src[:, split:])

        def quantize_w1(b, g, n):
            if g == 0:
                codes = wq_pool.tile([P, G1 * P], U32, name="w1_codes", align_bytes=64)
                scales = wq_pool.tile([P, G1 * P], U8, name="w1_scales", align_bytes=64)
                wq[b] = (codes, scales)
            codes, scales = wq[b]
            nc.vector.quantize_mx(
                out=codes[:, g * P : (g + n) * P].bitcast(FP8X4),
                scales=scales[:, g * P : (g + n) * P],
                in_=win[b][:, g : g + n].rearrange("p g c j -> p (g c j)"),
            )

        def quantize_x(g, lo, hi):
            if lo == 0:
                rawx[g, "in"] = xin_pool.tile([P, T, J], BF16, name="x_in", align_bytes=64)
            inter = rawx[g, "in"]
            mid = lo + (hi - lo) * 5 // 16
            nc.scalar.copy(out=inter[:, lo:mid], in_=rawx[g][:, :, lo:mid].rearrange("p j t -> p t j"))
            nc.vector.tensor_copy(out=inter[:, mid:hi], in_=rawx[g][:, :, mid:hi].rearrange("p j t -> p t j"))
            nc.vector.quantize_mx(
                out=xcodes[g][:, lo:hi].bitcast(FP8X4),
                scales=xscales[g][:, lo:hi],
                in_=inter[:, lo:hi].rearrange("p t j -> p (t j)"),
            )

        hs = {}

        def layer1(b, order):
            codes, scales = wq[b]
            acc = [acc_pool.tile([P, HALF], F32, name="acc") for s in range(2)]
            for g, s in order:
                cols = slice(g * P, (g + 1) * P)
                ts = slice(s * HALF, (s + 1) * HALF)
                nc.tensor.matmul_mx(
                    out=acc[s][:],
                    lhsT=codes[:, cols].bitcast(FP8X4),
                    lhsT_scale=scales[:, cols],
                    rhs=xcodes[g][:, ts].bitcast(FP8X4),
                    rhs_scale=xscales[g][:, ts],
                    start=(g == 0),
                    stop=(g == G1 - 1),
                )
            h = h_pool.tile([P, T], F32, name="h")
            for s in range(2):
                if b == 0 and s == 1:
                    nc.vector.tensor_scalar_max(h[:, HALF:T], acc[1][:], 0.0)
                else:
                    nc.scalar.activation(h[:, s * HALF : (s + 1) * HALF], acc[s][:], RELU)
            hs[b] = h

        def gather(b, v0, n, prods, ds):
            for d in ds:
                prod = prod_pool.tile([P, n], F32, name=f"prod{d}")
                nc.vector.tensor_tensor(
                    prod[:], hs[b][:].indirect(pos[d][:, v0 // 16 : (v0 + n) // 16]), gates[d][:, v0 : v0 + n], MULT
                )
                prods.append(prod)

        zts = {}

        def sum_transposed(b, prods, c0, engine_copy):
            g, bl = b // BG, b % BG
            if bl == 0:
                zts[g] = zts_pool.tile([P, NC, KP], BF16, name="zts")
            n = prods[0].shape[1] // P
            if n == NC:
                zt = zt_pool.tile([P, n, P], F32, name="zt")
                for c in range(n):
                    for d in range(D):
                        nc.tensor.matmul(
                            zt[:, c], prods[d][:, c * P : (c + 1) * P], ident[:],
                            start=(d == 0), stop=(d == D - 1), is_transpose=True,
                        )
                engine_copy(out=zts[g][:, c0 : c0 + n, bl * P : (bl + 1) * P], in_=zt[:])
            else:
                banks = [zt_pool.tile([P, P], F32, name="zt") for c in range(n)]
                for d in range(D):
                    for c in range(n):
                        nc.tensor.matmul(
                            banks[c][:], prods[d][:, c * P : (c + 1) * P], ident[:],
                            start=(d == 0), stop=(d == D - 1), is_transpose=True,
                        )
                for c in range(n):
                    engine_copy(out=zts[g][:, c0 + c, bl * P : (bl + 1) * P], in_=banks[c][:])

        zin = {}

        def untranspose_z(g, c, n, engine_copy):
            if (g, c) in ((0, 0), (1, 0), (1, 2), (1, 3)):
                zin[g] = zin_pool.tile([P, NC, P, J], BF16, name="z_in", align_bytes=64)
            zb = zb_pool.tile([P, n, 2, P], F32, name="zb")
            for i in range(n):
                words = zts[g][:, c + i].bitcast(F32)
                for u in range(2):
                    nc.tensor.transpose(zb[:, i, u], words[:, u::2], ident[:])
            engine_copy(
                out=zin[g][:, c : c + n].rearrange("p c v t -> p (c v t)").bitcast(F32).rearrange("p (c v u) -> p c v u", c=n, u=2),
                in_=zb[:].rearrange("p c u v -> p c v u"),
            )

        def quantize_z(g, c, n):
            nc.vector.quantize_mx(
                out=zcodes[g][:, c * P : (c + n) * P].bitcast(FP8X4),
                scales=zscales[g][:, c * P : (c + n) * P],
                in_=zin[g][:, c : c + n].rearrange("p c v t -> p (c v t)"),
            )

        w2in = []

        def interleave_w2():
            raw = rawx_pool.tile([P, G2, J, N], F32, name="raw_x")
            for g in range(G2):
                nc.sync.dma_start(out=raw[:, g], in_=w2[g * KP : (g + 1) * KP].rearrange("(p j) m -> p j m", j=J))
            inter = xin_pool.tile([P, G2, N, J], BF16, name="x_in", align_bytes=64)
            for g in range(G2):
                nc.scalar.copy(out=inter[:, g], in_=raw[:, g].rearrange("p j m -> p m j"))
            w2in.append(inter)

        def quantize_w2():
            nc.vector.quantize_mx(
                out=w2codes[:].bitcast(FP8X4),
                scales=w2scales[:],
                in_=w2in[0][:].rearrange("p g m j -> p (g m j)"),
            )

        out_v = out.rearrange("(m p) v -> p m v", p=P)

        def layer2(v0, n, m0, m1, engine_copy):
            acc = acc_pool.tile([P, m1 - m0, n], F32, name="acc")
            for m in range(m0, m1):
                for g in range(G2):
                    nc.tensor.matmul_mx(
                        out=acc[:, m - m0],
                        lhsT=w2codes[:, g * N + m * P : g * N + (m + 1) * P].bitcast(FP8X4),
                        lhsT_scale=w2scales[:, g * N + m * P : g * N + (m + 1) * P],
                        rhs=zcodes[g][:, v0 : v0 + n].bitcast(FP8X4),
                        rhs_scale=zscales[g][:, v0 : v0 + n],
                        start=(g == 0),
                        stop=(g == G2 - 1),
                    )
            res = res_pool.tile([P, m1 - m0, n], F32, name="res")
            engine_copy(out=res[:], in_=acc[:])
            nc.sync.dma_start(out=out_v[:, m0:m1, v0 : v0 + n], in_=res[:])

        interleave_w1(0, 0)
        interleave_w1(0, 1)
        for g in range(G1):
            for half in range(2):
                quantize_x(g, half * HALF, (half + 1) * HALF)
            if g == 1:
                quantize_w1(0, 0, 2)
        for g in (2, 3):
            interleave_w1(0, g, split=80)
            quantize_w1(0, g, 1)
        layer1(0, [(g, s) for g in range(G1) for s in range(2)])

        halves_first = [(g, s) for s in range(2) for g in range(G1)]
        for b in range(NB - 1):
            if b + 2 < NB:
                for g in range(G1):
                    load_w1_pass(b + 2, g)
            for g in range(G1):
                interleave_w1(b + 1, g)
            prods = []
            gather(b, 0, V, prods, range(0, 2))
            if b == 0:
                quantize_w1(1, 0, 2)
                gather(b, 0, V, prods, range(2, 4))
                quantize_w1(1, 2, 2)
                layer1(1, [(g, s) for g in range(G1) for s in range(2)])
                gather(b, 0, V, prods, range(4, D))
            else:
                quantize_w1(b + 1, 0, 4)
                layer1(b + 1, halves_first)
                gather(b, 0, V, prods, range(2, D))
            if b == 3:
                interleave_w2()
            if b == 4:
                for c in range(0, NC, 2):
                    untranspose_z(0, c, 2, nc.scalar.copy)
            if b == 5:
                quantize_z(0, 0, NC)
                quantize_w2()
            sum_transposed(b, prods, 0, nc.scalar.copy)

        b = NB - 1
        p0, p1, p2 = [], [], []
        gather(b, 0, 2 * P, p0, range(D))
        sum_transposed(b, p0, 0, nc.scalar.copy)
        gather(b, 2 * P, P, p1, range(D))
        untranspose_z(1, 0, 2, nc.scalar.copy)
        sum_transposed(b, p1, 2, nc.scalar.copy)
        gather(b, 3 * P, P, p2, range(0, 2))
        quantize_z(1, 0, 2)
        gather(b, 3 * P, P, p2, range(2, 5))
        untranspose_z(1, 2, 1, nc.scalar.copy)
        quantize_z(1, 2, 1)
        gather(b, 3 * P, P, p2, range(5, D))
        sum_transposed(b, p2, 3, nc.vector.tensor_copy)
        untranspose_z(1, 3, 1, nc.scalar.copy)
        layer2(0, 2 * P, 0, 2, nc.scalar.copy)
        layer2(0, 2 * P, 2, 4, nc.scalar.copy)
        quantize_z(1, 3, 1)
        layer2(2 * P, P, 0, 4, nc.vector.tensor_copy)
        layer2(3 * P, P, 0, 2, nc.scalar.copy)
        layer2(3 * P, P, 2, 4, nc.vector.tensor_copy)
